import numpy as np
import ml_dtypes


def mxq(x, axis, fmt="e4m3"):
    dtype, down = {"e4m3": (ml_dtypes.float8_e4m3fn, 7), "e5m2": (ml_dtypes.float8_e5m2, 14)}[fmt]
    v = np.moveaxis(np.asarray(x, np.float32).astype(ml_dtypes.bfloat16).astype(np.float64), axis, -1)
    blocks = v.reshape(v.shape[:-1] + (-1, 32))
    amax = np.abs(blocks).max(-1, keepdims=True)
    byte = np.maximum(np.where(amax > 0, np.frexp(amax)[1] - 1 + 127, 0) - down, 1)
    scale = np.exp2(byte - 127.0)
    codes = (blocks / scale).astype(np.float32).astype(dtype).astype(np.float64)
    return np.moveaxis((codes * scale).reshape(v.shape), -1, axis)


WIDE = False


def mx_kscale(k):
    if not WIDE:
        return np.ones(k)
    levels = np.array([10, -10, 5, -5, 0])
    if k % 512:
        return np.exp2(np.random.permutation(np.resize(levels, k // 32))).repeat(32)
    a = np.empty((k // 512, 16))
    for p in range(k // 512):
        a[p, :8] = np.random.permutation(np.resize(levels, 8))
        for g in range(8):
            far = levels[np.abs(levels - a[p, g]) >= 10]
            a[p, g + 8] = far[np.random.randint(len(far))]
    return np.exp2(a.ravel()).repeat(32)


BF16 = ml_dtypes.bfloat16


def bf(x):
    return np.asarray(x, np.float32).astype(BF16)


def f64(x):
    return np.asarray(x).astype(np.float64)


E2M1 = np.array([0.0, 0.5, 1.0, 1.5, 2.0, 3.0, 4.0, 6.0, -0.0, -0.5, -1.0, -1.5, -2.0, -3.0, -4.0, -6.0])


def pack_weight(w, fmt):
    k, n = w.shape
    w = f64(bf(w)).reshape(k // 32, 32, n)
    amax = np.abs(w).max(1)
    if fmt == "e4m3":
        byte = np.frexp(amax)[1] - 1 + 127 - 7
    else:
        mant, ex = np.frexp(amax / 6.0)
        byte = np.where(mant > 0.5, ex, ex - 1) + 127
    byte = np.clip(np.where(amax > 0, byte, 1), 1, 254)
    scaled = (w * np.exp2(127.0 - byte)[:, None, :]).reshape(k, n).astype(np.float32)
    by_word = np.ascontiguousarray(scaled.reshape(k // 512, 128, 4, n).transpose(0, 1, 3, 2))
    if fmt == "e4m3":
        words = by_word.astype(ml_dtypes.float8_e4m3fn).view(np.uint8)
    else:
        c = by_word.astype(ml_dtypes.float4_e2m1fn).view(np.uint8) & 0xF
        words = c[..., 0::2] | (c[..., 1::2] << 4)
    return np.ascontiguousarray(words), np.ascontiguousarray(byte.astype(np.uint8).reshape(k // 512, 16, n))


def unpack_weight(words, scales, fmt):
    g, p, n, _ = words.shape
    if fmt == "e4m3":
        vals = np.ascontiguousarray(words).view(ml_dtypes.float8_e4m3fn).astype(np.float64)
    else:
        nib = np.empty((g, p, n, 4), np.uint8)
        nib[..., 0::2] = words & 0xF
        nib[..., 1::2] = words >> 4
        vals = E2M1[nib]
    vals = vals * np.repeat(np.exp2(scales.astype(np.float64) - 127.0), 8, axis=1)[..., None]
    return vals.transpose(0, 1, 3, 2).reshape(g * 512, n)
def pack4(w):
    words, scales = pack_weight(w, "e2m1")
    return words.reshape(words.shape[0], 128, -1), scales


def unpack4(words, scales):
    return unpack_weight(words.reshape(words.shape[0], 128, -1, 2), scales, "e2m1")


G, K, C, P = 2048, 1024, 512, 1024


def silu(v):
    return 0.5 * v * (1.0 + np.tanh(0.5 * v))


def draw0():
    s, t = mx_kscale(K), mx_kscale(G)
    gate_words, gate_scales = pack4(np.random.standard_normal((K, C)) / np.sqrt(K) / s[:, None])
    value_words, value_scales = pack4(np.random.standard_normal((K, C)) / np.sqrt(K) / s[:, None])
    mix_words, mix_scales = pack4(np.random.standard_normal((G, P)) / np.sqrt(G) / t[:, None])
    return {"state": bf(np.random.standard_normal((G, K)) * s),
            "gate_words": gate_words, "gate_scales": gate_scales,
            "gate_bias": bf(0.3 * np.random.standard_normal(C)),
            "sun": bf(np.random.uniform(0.0, 1.0, G)),
            "sun_gain": bf(0.5 * np.random.standard_normal(C)),
            "value_words": value_words, "value_scales": value_scales,
            "value_bias": bf(0.3 * np.random.standard_normal(C)),
            "area": bf(np.random.uniform(0.5, 1.5, G) * t),
            "mix_words": mix_words, "mix_scales": mix_scales,
            "mesh": bf(np.random.standard_normal((P, C))),
            "gain": bf(1.0 + 0.1 * np.random.standard_normal(C))}


def core(state, gate_words, gate_scales, gate_bias, sun, sun_gain, value_words, value_scales, value_bias, area, mix_words, mix_scales, mesh, gain):
    xq = mxq(f64(state), 1, "e4m3")
    a = (xq @ unpack4(gate_words, gate_scales)) + f64(gate_bias) + f64(sun)[:, None] * f64(sun_gain)
    v = (xq @ unpack4(value_words, value_scales)) + f64(value_bias)
    h = silu(a) * v * f64(area)[:, None]
    z = unpack4(mix_words, mix_scales).T @ mxq(h, 0, "e4m3")
    rms = np.sqrt(np.mean(z * z, axis=1, keepdims=True))
    return f64(mesh) + z / rms * f64(gain)


def e4m3fn_bytes(y):
    return np.clip(np.asarray(y, np.float64), -448.0, 448.0).astype(np.float32).astype(ml_dtypes.float8_e4m3fn).view(np.uint8)


def e4m3fn_values(b):
    return np.asarray(b, np.uint8).view(ml_dtypes.float8_e4m3fn).astype(np.float64)


def setup_inputs():
    d = draw0()
    x0 = np.asarray(d['state']).astype(np.float64)
    s = (np.max(np.abs(x0), axis=(0,), keepdims=True) / 448.0).astype(np.float32)
    out = {}
    for k, v in d.items():
        if k == 'state':
            out['state_bytes'] = e4m3fn_bytes(x0 / s.astype(np.float64))
            out['state_scale'] = s
        else:
            out[k] = v
    return out


def reference(state_bytes, state_scale, gate_words, gate_scales, gate_bias, sun, sun_gain, value_words, value_scales, value_bias, area, mix_words, mix_scales, mesh, gain):
    return core(e4m3fn_values(state_bytes) * state_scale.astype(np.float64), gate_words, gate_scales, gate_bias, sun, sun_gain, value_words, value_scales, value_bias, area, mix_words, mix_scales, mesh, gain)

@@ -1,0 +1,403 @@
+from contextlib import ExitStack
+
+import concourse.mybir as mybir
+from concourse.masks import make_identity
+
+G, K, C, P = 2048, 1024, 512, 1024
+FLOPS = 2 * G * K * C * 2 + 2 * G * P * C
+
+F32 = mybir.dt.float32
+BF16 = mybir.dt.bfloat16
+U8 = mybir.dt.uint8
+U32 = mybir.dt.uint32
+I32 = mybir.dt.int32
+E4M3 = mybir.dt.float8_e4m3fn
+E4M3X4 = mybir.dt.float8_e4m3fn_x4
+E2M1X4 = mybir.dt.float4_e2m1fn_x4
+ALU = mybir.AluOpType
+ACT = mybir.ActivationFunctionType
+
+NG = 4
+
+
+def tile_grid_to_mesh_mixing_f1_kernel(
+    tc, state_bytes, state_scale, gate_words, gate_scales, gate_bias, sun, sun_gain,
+    value_words, value_scales, value_bias, area, mix_words, mix_scales, mesh, gain, out,
+):
+    nc = tc.nc
+    with ExitStack() as ctx:
+        keep = ctx.enter_context(tc.tile_pool(name="keep", bufs=1))
+        work = ctx.enter_context(tc.tile_pool(name="work", bufs=2))
+        psum = ctx.enter_context(tc.psum_pool(name="psum", bufs=1))
+
+        state_sb = [keep.tile([128, 4, K], U8, name=f"state{g}", align_bytes=64) for g in range(NG)]
+        scale_b = keep.tile([128, K], F32, name="scale_b")
+        gate_w = keep.tile([128, 2, 2 * C], U8, name="gate_w", align_bytes=64)
+        value_w = keep.tile([128, 2, 2 * C], U8, name="value_w", align_bytes=64)
+        gate_s = keep.tile([128, 2, C], U8, name="gate_s", align_bytes=64)
+        value_s = keep.tile([128, 2, C], U8, name="value_s", align_bytes=64)
+        mix_w = keep.tile([128, NG, 2 * P], U8, name="mix_w", align_bytes=64)
+        mix_s = keep.tile([128, NG, P], U8, name="mix_s", align_bytes=64)
+        mesh_sb = keep.tile([128, 8, C], BF16, name="mesh_sb")
+        ident = keep.tile([128, 128], F32, name="ident")
+        ident_bf = keep.tile([128, 16], BF16, name="ident_bf")
+        ones = keep.tile([128, 128], BF16, name="ones")
+        vec_rows = keep.tile([128, 128], BF16, name="vec_rows")
+        row0 = keep.tile([128, G + C], BF16, name="row0")
+        sun_b = keep.tile([128, G], F32, name="sun_b")
+        gain_b = keep.tile([128, C], F32, name="gain_b")
+        cols = keep.tile([128, 16], F32, name="cols")
+        area_bf = keep.tile([128, NG, 4], BF16, name="area_bf")
+        area_c = keep.tile([128, NG, 4], F32, name="area_c")
+        dummy = keep.tile([128, 1], F32, name="dummy")
+        mhalf = keep.tile([128, 1], F32, name="mhalf")
+        h_codes = keep.tile([128, NG, C], U32, name="h_codes", align_bytes=64)
+        h_scales = keep.tile([128, NG, C], U8, name="h_scales", align_bytes=64)
+
+        def load_state(g, t0, t1):
+            src = state_bytes[512 * g : 512 * (g + 1), :].rearrange("(p t) k -> p t k", t=4)
+            nc.sync.dma_start(out=state_sb[g][:, t0:t1, :], in_=src[:, t0:t1, :])
+
+        def load_scales(tile, dram):
+            src = dram.rearrange("g (q r) n -> r q g n", r=4)
+            for r in range(4):
+                nc.sync.dma_start(out=tile[r:128:32, :, :].bitcast(I32), in_=src[r].bitcast(I32))
+
+        load_state(0, 0, 1)
+        nc.scalar.dma_start(out=scale_b[:], in_=state_scale.rearrange("o k -> (o k)").partition_broadcast(128))
+        load_state(0, 1, 2)
+        load_state(0, 2, 4)
+        nc.vector.memset(dummy[:], 0.0)
+        nc.scalar.activation(out=dummy[:], in_=dummy[:], func=ACT.Silu)
+        nc.vector.memset(gate_s[:].rearrange("p g n -> p (g n)").bitcast(I32), 0)
+        nc.vector.memset(value_s[:].rearrange("p g n -> p (g n)").bitcast(I32), 0)
+        nc.vector.memset(vec_rows[:].bitcast(U32), 0)
+        nc.vector.memset(row0[:].bitcast(U32), 0)
+        nc.vector.memset(mix_s[:].rearrange("p g n -> p (g n)").bitcast(I32), 0)
+        make_identity(nc, ident[:])
+        nc.gpsimd.dma_start(out=vec_rows[0:4, :], in_=gate_bias.rearrange("(j c) -> j c", c=128))
+        nc.gpsimd.dma_start(out=vec_rows[4:8, :], in_=sun_gain.rearrange("(j c) -> j c", c=128))
+        nc.gpsimd.dma_start(out=vec_rows[8:12, :], in_=value_bias.rearrange("(j c) -> j c", c=128))
+        nc.gpsimd.dma_start(out=row0[0:1, 0:G], in_=sun.rearrange("(o g) -> o g", o=1))
+        nc.gpsimd.memset(ones[:], 1.0)
+        nc.gpsimd.tensor_copy(out=ident_bf[:], in_=ident[:, 0:16])
+        nc.gpsimd.dma_start(out=row0[0:1, G : G + C], in_=gain.rearrange("(o g) -> o g", o=1))
+        nc.gpsimd.dma_start(out=area_bf[:], in_=area.rearrange("(g p t) -> p g t", p=128, t=4))
+        nc.gpsimd.memset(mhalf[:], -0.5)
+        nc.gpsimd.tensor_copy(out=area_c[:], in_=area_bf[:])
+
+        load_scales(gate_s, gate_scales)
+        load_scales(value_s, value_scales)
+        nc.sync.dma_start(out=gate_w[:], in_=gate_words.rearrange("g p n -> p g n"))
+        nc.sync.dma_start(out=value_w[:], in_=value_words.rearrange("g p n -> p g n"))
+        load_state(1, 0, 4)
+        load_state(2, 0, 4)
+        load_scales(mix_s, mix_scales)
+        load_state(3, 0, 4)
+        nc.sync.dma_start(out=mix_w[:], in_=mix_words.rearrange("g p n -> p g n"))
+        nc.sync.dma_start(out=mesh_sb[:], in_=mesh.rearrange("(m p) c -> p m c", p=128))
+
+        x_bank, e_bank, h_bank = 2, 4, 2
+
+        def bank(tag, n, name):
+            return psum.tile([128, 512], F32, tag=tag, bufs=n, name=name)
+
+        xw, xg, xq, xs = {}, {}, {}, {}
+
+        def widen(g, t):
+            w = work.tile([128, K], BF16, tag="xw", bufs=6, name=f"xw{g}_{t}")
+            nc.vector.tensor_tensor(out=w[:], in0=state_sb[g][:, t, :].bitcast(E4M3), in1=scale_b[:], op=ALU.mult)
+            xw[g, t] = w
+
+        def turn(g, tp):
+            banks = []
+            for kg in range(2):
+                b = bank("x", x_bank, f"xt{g}_{tp}_{kg}")
+                bv = b[:].rearrange("p (t u r) -> p t u r", t=2, u=2)
+                for t in range(2):
+                    words = xw[g, 2 * tp + t][:].bitcast(F32)
+                    for u in range(2):
+                        nc.tensor.transpose(bv[:, t, u, :], words[:, 256 * kg + u : 256 * (kg + 1) : 2], ident[:])
+                banks.append(bv)
+            return banks
+
+        def take(g, tp, banks):
+            for kg in range(2):
+                if tp == 0:
+                    xg[g, kg] = work.tile([128, 512, 4], BF16, tag=f"xg{kg}", bufs=2, name=f"xg{g}_{kg}", align_bytes=64)
+                dst = xg[g, kg][:, 256 * tp : 256 * (tp + 1), :].rearrange("p c j -> p (c j)").bitcast(F32)
+                nc.scalar.copy(
+                    out=dst.rearrange("p (t r u) -> p t r u", t=2, u=2),
+                    in_=banks[kg].rearrange("p t u r -> p t r u"),
+                )
+
+        def quant_x(g, kg):
+            if kg == 0:
+                xq[g] = work.tile([128, 2, 512], U32, tag="xq", bufs=2, name=f"xq{g}", align_bytes=64)
+                xs[g] = work.tile([128, 2, 512], U8, tag="xs", bufs=2, name=f"xs{g}", align_bytes=64)
+            nc.vector.quantize_mx(
+                out=xq[g][:, kg, :].bitcast(E4M3X4), scales=xs[g][:, kg, :],
+                in_=xg[g, kg][:].rearrange("p c j -> p (c j)"),
+            )
+
+        eb, ub, ah, sh, hh = {}, {}, {}, {}, {}
+
+        def encode(g, j):
+            for store, words, scales, nm in ((eb, gate_w, gate_s, "e"), (ub, value_w, value_s, "u")):
+                b = bank("e", e_bank, f"{nm}{g}_{j}")
+                for kg in range(2):
+                    nc.tensor.matmul_mx(
+                        out=b[:],
+                        lhsT=words[:, kg, 256 * j : 256 * (j + 1)].bitcast(E2M1X4),
+                        lhsT_scale=scales[:, kg, 128 * j : 128 * (j + 1)],
+                        rhs=xq[g][:, kg, :].bitcast(E4M3X4),
+                        rhs_scale=xs[g][:, kg, :],
+                        start=(kg == 0), stop=(kg == 1),
+                    )
+                store[g, j] = b
+
+        def add_sun(g, j):
+            a = work.tile([128, 512], F32, tag="a", bufs=3, name=f"a{g}_{j}")
+            nc.vector.scalar_tensor_tensor(
+                out=a[:], in0=sun_b[:, 512 * g : 512 * (g + 1)], scalar=cols[:, 4 + j : 5 + j], in1=eb[g, j][:],
+                op0=ALU.mult, op1=ALU.add,
+            )
+            ah[g, j] = a
+
+        def gate(g, j):
+            s = work.tile([128, 512], F32, tag="s", bufs=3, name=f"s{g}_{j}")
+            nc.scalar.activation(out=s[:], in_=ah[g, j][:], func=ACT.Silu, bias=cols[:, j : j + 1])
+            sh[g, j] = s
+
+        def product(g, j):
+            h = work.tile([128, 512], F32, tag="hT", bufs=6, name=f"hT{g}_{j}")
+            nc.vector.scalar_tensor_tensor(
+                out=h[:], in0=ub[g, j][:], scalar=cols[:, 8 + j : 9 + j], in1=sh[g, j][:], op0=ALU.add, op1=ALU.mult,
+            )
+            hh[g, j] = h
+
+        hbank, hb, hi = {}, {}, {}
+
+        def turn_h(g, hf):
+            for tp in range(2):
+                b = bank("h", h_bank, f"hp{g}_{hf}_{tp}")
+                bv = b[:].rearrange("p (t c) -> p t c", t=2)
+                for t in range(2):
+                    for jj in range(2):
+                        tt = 2 * tp + t
+                        nc.tensor.transpose(
+                            bv[:, t, 128 * jj : 128 * (jj + 1)],
+                            hh[g, 2 * hf + jj][:, 128 * tt : 128 * (tt + 1)], ident[:],
+                        )
+                hbank[g, hf, tp] = bv
+
+        def take_h(g, hf):
+            hb[g, hf] = work.tile([128, 4, 256], BF16, tag="hb", bufs=2, name=f"hb{g}_{hf}")
+            for t in range(4):
+                nc.scalar.activation(
+                    out=hb[g, hf][:, t, :], in_=hbank[g, hf, t // 2][:, t % 2, :], func=ACT.Copy,
+                    scale=area_c[:, g, t : t + 1],
+                )
+
+        def turn_direct(g, j):
+            b = bank("h", h_bank, f"hd{g}_{j}")
+            bv = b[:].rearrange("p (t c) -> p t c", t=4)
+            for t in range(4):
+                nc.tensor.transpose(bv[:, t, :], hh[g, j][:, 128 * t : 128 * (t + 1)], ident[:])
+            hbank[g, j] = bv
+
+        def take_direct(g, j):
+            hf = j // 2
+            if j % 2 == 0:
+                hi[g, hf] = work.tile([128, 256, 4], BF16, tag="hi", bufs=2, name=f"hi{g}_{hf}", align_bytes=64)
+            nc.vector.tensor_tensor(
+                out=hi[g, hf][:, 128 * (j % 2) : 128 * (j % 2 + 1), :],
+                in0=hbank[g, j].rearrange("p t c -> p c t"),
+                in1=area_c[:, g, :].unsqueeze(1).to_broadcast([128, 128, 4]),
+                op=ALU.mult,
+            )
+
+        def weave_h(g, hf, engine):
+            hi[g, hf] = work.tile([128, 256, 4], BF16, tag="hi", bufs=2, name=f"hi{g}_{hf}", align_bytes=64)
+            dst = hi[g, hf][:].rearrange("p (c i) t -> p c t i", i=4)
+            src = hb[g, hf][:].rearrange("p t (c i) -> p c t i", i=4)
+            if engine == "v":
+                nc.vector.tensor_copy(out=dst, in_=src)
+            else:
+                nc.scalar.copy(out=dst, in_=src)
+
+        def quant_h(g, hf):
+            cs = slice(256 * hf, 256 * (hf + 1))
+            nc.vector.quantize_mx(
+                out=h_codes[:, g, cs].bitcast(E4M3X4), scales=h_scales[:, g, cs],
+                in_=hi[g, hf][:].rearrange("p c t -> p (c t)"),
+            )
+
+        zb = {}
+
+        def mix(m, g, tag, n):
+            if g == 0:
+                zb[m] = bank(tag, n, f"z{m}")
+            nc.tensor.matmul_mx(
+                out=zb[m][:],
+                lhsT=mix_w[:, g, 256 * m : 256 * (m + 1)].bitcast(E2M1X4),
+                lhsT_scale=mix_s[:, g, 128 * m : 128 * (m + 1)],
+                rhs=h_codes[:, g, :].bitcast(E4M3X4),
+                rhs_scale=h_scales[:, g, :],
+                start=(g == 0), stop=(g == NG - 1),
+            )
+
+        rinvs = {}
+
+        def norm(m):
+            sq = work.tile([128, 512], BF16, tag="sq", bufs=2, name=f"sq{m}")
+            ssq = work.tile([128, 1], F32, tag="ssq", bufs=8, name=f"ssq{m}")
+            rinv = work.tile([128, 1], F32, tag="rinv", bufs=8, name=f"rinv{m}")
+            nc.scalar.activation(out=sq[:], in_=zb[m][:], func=ACT.Square, accum_out=ssq[:])
+            nc.gpsimd.tensor_tensor(out=rinv[:], in0=ssq[:], in1=mhalf[:], op=ALU.pow)
+            rinvs[m] = rinv
+
+        def scale_z(m):
+            y = work.tile([128, 512], F32, tag="y", bufs=4, name=f"y{m}")
+            o = work.tile([128, 512], F32, tag="o", bufs=8, name=f"o{m}")
+            nc.vector.scalar_tensor_tensor(
+                out=y[:], in0=zb[m][:], scalar=rinvs[m][:], in1=gain_b[:], op0=ALU.mult, op1=ALU.mult,
+            )
+            ys[m] = y
+            outs[m] = o
+
+        ys, outs = {}, {}
+
+        def add_mesh(m, eng):
+            eng.tensor_tensor(out=outs[m][:], in0=ys[m][:], in1=mesh_sb[:, m, :], op=ALU.add)
+            nc.sync.dma_start(out=out[128 * m : 128 * (m + 1), :], in_=outs[m][:])
+
+        def spread_vectors():
+            ps = bank("h", h_bank, "vec_ps")
+            nc.tensor.matmul(ps[:, 0:16], lhsT=vec_rows[:], rhs=ident_bf[:], start=True, stop=True)
+            nc.scalar.copy(out=cols[:], in_=ps[:, 0:16])
+            for g in range(NG):
+                ps = bank("e", e_bank, f"sun_ps{g}")
+                nc.tensor.matmul(ps[:], lhsT=ones[:], rhs=row0[:, 512 * g : 512 * (g + 1)], start=True, stop=True)
+                nc.scalar.copy(
+                    out=sun_b[:, 512 * g : 512 * (g + 1)].rearrange("p (t q) -> p t q", t=4),
+                    in_=ps[:].rearrange("p (q t) -> p t q", t=4),
+                )
+            ps = bank("h", h_bank, "gain_ps")
+            nc.tensor.matmul(ps[:], lhsT=ones[:], rhs=row0[:, G : G + C], start=True, stop=True)
+            nc.scalar.activation(out=gain_b[:], in_=ps[:], func=ACT.Copy, scale=math_sqrt_c())
+
+        with tc.manual_schedule(engines={mybir.EngineType.PE, mybir.EngineType.DVE, mybir.EngineType.Activation}):
+            widen(0, 0)
+            widen(0, 1)
+            b = turn(0, 0)
+            take(0, 0, b)
+            widen(0, 2)
+            widen(0, 3)
+            b = turn(0, 1)
+            take(0, 1, b)
+            spread_vectors()
+            widen(1, 0)
+            quant_x(0, 0)
+            widen(1, 1)
+            quant_x(0, 1)
+            b = turn(1, 0)
+            take(1, 0, b)
+            encode(0, 0)
+            for g in range(NG - 1):
+                n, n2 = g + 1, g + 2
+                encode(g, 1)
+                add_sun(g, 0)
+                gate(g, 0)
+                if g > 0:
+                    turn_h(g - 1, 1)
+                    take_h(g - 1, 1)
+                widen(n, 2)
+                add_sun(g, 1)
+                gate(g, 1)
+                product(g, 0)
+                if g > 0:
+                    weave_h(g - 1, 1, "a")
+                encode(g, 2)
+                widen(n, 3)
+                product(g, 1)
+                b = turn(n, 1)
+                encode(g, 3)
+                add_sun(g, 2)
+                gate(g, 2)
+                take(n, 1, b)
+                if n2 < NG:
+                    widen(n2, 0)
+                add_sun(g, 3)
+                gate(g, 3)
+                turn_h(g, 0)
+                take_h(g, 0)
+                if g > 0:
+                    quant_h(g - 1, 1)
+                quant_x(n, 0)
+                quant_x(n, 1)
+                product(g, 2)
+                weave_h(g, 0, "a" if n2 < NG else "v")
+                encode(n, 0)
+                if n2 < NG:
+                    widen(n2, 1)
+                product(g, 3)
+                if n2 < NG:
+                    b = turn(n2, 0)
+                    take(n2, 0, b)
+                quant_h(g, 0)
+            g = NG - 1
+            encode(g, 1)
+            turn_h(g - 1, 1)
+            add_sun(g, 0)
+            gate(g, 0)
+            add_sun(g, 1)
+            take_h(g - 1, 1)
+            gate(g, 1)
+            product(g, 0)
+            for m in range(2):
+                for gg in range(2):
+                    mix(m, gg, "x", x_bank)
+            encode(g, 2)
+            weave_h(g - 1, 1, "v")
+            product(g, 1)
+            add_sun(g, 2)
+            gate(g, 2)
+            encode(g, 3)
+            turn_direct(g, 0)
+            turn_direct(g, 1)
+            quant_h(g - 1, 1)
+            add_sun(g, 3)
+            gate(g, 3)
+            take_direct(g, 0)
+            product(g, 2)
+            for m in range(2):
+                mix(m, 2, "x", x_bank)
+            turn_direct(g, 2)
+            for gg in range(3):
+                mix(2, gg, "e", e_bank)
+            take_direct(g, 1)
+            product(g, 3)
+            quant_h(g, 0)
+            turn_direct(g, 3)
+            take_direct(g, 2)
+            for gg in range(3):
+                mix(3, gg, "e", e_bank)
+            take_direct(g, 3)
+            quant_h(g, 1)
+            for m in range(4):
+                mix(m, 3, "e", e_bank)
+            for m in range(4, 8):
+                for gg in range(NG):
+                    mix(m, gg, "e" if m < 6 else "h", e_bank if m < 6 else h_bank)
+            ahead = 3
+            for m in range(8 + ahead):
+                if m < 8:
+                    norm(m)
+                if m >= ahead:
+                    scale_z(m - ahead)
+                    add_mesh(m - ahead, nc.gpsimd if (m - ahead) % 2 == 1 else nc.vector)
+
+
+def math_sqrt_c():
+    return float(C) ** 0.5

@@ -19,6 +19,240 @@ ACT = mybir.ActivationFunctionType
 
 NG = 4
 
+PLAN = [
+    ("widen", 0, 0),
+    ("spread_sun", 0),
+    ("cast_s", 1, 1, 1),
+    ("widen", 0, 1),
+    ("widen", 0, 2),
+    ("cast_s", 1, 1, 3),
+    ("widen", 0, 3),
+    ("turn", 0, 0),
+    ("widen", 1, 2),
+    ("take", 0, 0),
+    ("widen", 1, 0),
+    ("turn", 0, 1),
+    ("cast_s", 1, 1, 0),
+    ("cast_s", 1, 1, 2),
+    ("take", 0, 1),
+    ("widen", 1, 1),
+    ("turn_s", 1, 1, 1),
+    ("widen", 1, 3),
+    ("turn_s", 1, 1, 0),
+    ("quant_x", 0, 0),
+    ("widen", 2, 1),
+    ("take_s", 1, 1, 1),
+    ("widen", 2, 3),
+    ("take_s", 1, 1, 0),
+    ("quant_x", 0, 1),
+    ("spread_vectors",),
+    ("encode", 0, 0, "e"),
+    ("encode", 0, 1, "e"),
+    ("encode", 0, 3, "e"),
+    ("encode", 0, 2, "e"),
+    ("widen", 2, 0),
+    ("turn", 1, 1),
+    ("turn", 1, 0),
+    ("add_sun", 0, 0),
+    ("weave_x", 1, 1, "a"),
+    ("take", 1, 1),
+    ("add_sun", 0, 1),
+    ("encode", 0, 3, "u"),
+    ("add_sun", 0, 3),
+    ("take", 1, 0),
+    ("widen", 3, 0),
+    ("quant_x", 1, 1),
+    ("encode", 0, 2, "u"),
+    ("turn", 2, 0),
+    ("add_sun", 0, 2),
+    ("quant_x", 1, 0),
+    ("encode", 1, 3, "e"),
+    ("gate", 0, 3),
+    ("encode", 1, 2, "e"),
+    ("gate", 0, 0),
+    ("product", 0, 3),
+    ("gate", 0, 2),
+    ("product", 0, 2),
+    ("add_sun", 1, 3),
+    ("turn_h", 0, 1, 1),
+    ("turn_h", 0, 1, 0),
+    ("take", 2, 0),
+    ("encode", 0, 1, "u"),
+    ("gate", 0, 1),
+    ("take_h", 0, 1, 0),
+    ("widen", 2, 2),
+    ("add_sun", 1, 2),
+    ("encode", 0, 0, "u"),
+    ("take_h", 0, 1, 1),
+    ("product", 0, 1),
+    ("gate", 1, 3),
+    ("product", 0, 0),
+    ("weave_h", 0, 1, "a"),
+    ("encode", 1, 0, "e"),
+    ("encode", 1, 1, "e"),
+    ("add_sun", 1, 0),
+    ("turn", 2, 1),
+    ("turn_h", 0, 0, 1),
+    ("turn_h", 0, 0, 0),
+    ("add_sun", 1, 1),
+    ("take", 2, 1),
+    ("take_h", 0, 0, 1),
+    ("take_h", 0, 0, 0),
+    ("encode", 1, 3, "u"),
+    ("widen", 3, 2),
+    ("gate", 1, 2),
+    ("widen", 3, 1),
+    ("encode", 1, 2, "u"),
+    ("encode", 1, 0, "u"),
+    ("encode", 1, 1, "u"),
+    ("quant_x", 2, 0),
+    ("product", 1, 3),
+    ("gate", 1, 0),
+    ("product", 1, 2),
+    ("turn", 3, 0),
+    ("turn_h", 1, 1, 0),
+    ("gate", 1, 1),
+    ("weave_h", 0, 0, "a"),
+    ("quant_x", 2, 1),
+    ("encode", 2, 1, "e"),
+    ("product", 1, 0),
+    ("product", 1, 1),
+    ("take", 3, 0),
+    ("add_sun", 2, 1),
+    ("encode", 2, 2, "e"),
+    ("add_sun", 2, 2),
+    ("widen", 3, 3),
+    ("encode", 2, 0, "e"),
+    ("take_h", 1, 1, 0),
+    ("encode", 2, 3, "e"),
+    ("gate", 2, 1),
+    ("turn_h", 1, 0, 0),
+    ("add_sun", 2, 0),
+    ("gate", 2, 2),
+    ("take_h", 1, 0, 0),
+    ("quant_h", 0, 0),
+    ("add_sun", 2, 3),
+    ("turn_h", 1, 1, 1),
+    ("turn", 3, 1),
+    ("take", 3, 1),
+    ("gate", 2, 3),
+    ("encode", 2, 3, "u"),
+    ("quant_x", 3, 0),
+    ("take_h", 1, 1, 1),
+    ("encode", 2, 2, "u"),
+    ("turn_h", 1, 0, 1),
+    ("take_h", 1, 0, 1),
+    ("quant_x", 3, 1),
+    ("product", 2, 3),
+    ("encode", 3, 1, "e"),
+    ("product", 2, 2),
+    ("encode", 2, 0, "u"),
+    ("gate", 2, 0),
+    ("encode", 3, 2, "e"),
+    ("encode", 2, 1, "u"),
+    ("turn_h", 2, 1, 0),
+    ("turn_h", 2, 1, 1),
+    ("weave_h", 1, 1, "a"),
+    ("take_h", 2, 1, 0),
+    ("add_sun", 3, 1),
+    ("take_h", 2, 1, 1),
+    ("product", 2, 0),
+    ("product", 2, 1),
+    ("encode", 3, 0, "e"),
+    ("add_sun", 3, 2),
+    ("quant_h", 0, 1),
+    ("encode", 3, 3, "e"),
+    ("quant_h", 1, 1),
+    ("add_sun", 3, 0),
+    ("add_sun", 3, 3),
+    ("gate", 3, 2),
+    ("gate", 3, 1),
+    ("gate", 3, 0),
+    ("encode", 3, 2, "u"),
+    ("product", 3, 2),
+    ("gate", 3, 3),
+    ("encode", 3, 3, "u"),
+    ("turn_h", 2, 0, 0),
+    ("turn_direct", 3, 2),
+    ("encode", 3, 1, "u"),
+    ("take_h", 2, 0, 0),
+    ("mix", 1, 0),
+    ("product", 3, 3),
+    ("weave_h", 1, 0, "a"),
+    ("turn_h", 2, 0, 1),
+    ("take_direct", 3, 2),
+    ("turn_direct", 3, 3),
+    ("take_h", 2, 0, 1),
+    ("encode", 3, 0, "u"),
+    ("mix", 2, 0),
+    ("mix", 3, 0),
+    ("weave_h", 2, 1, "a"),
+    ("product", 3, 1),
+    ("turn_direct", 3, 1),
+    ("take_direct", 3, 3),
+    ("product", 3, 0),
+    ("turn_direct", 3, 0),
+    ("mix", 5, 0),
+    ("quant_h", 1, 0),
+    ("weave_h", 2, 0, "a"),
+    ("mix", 1, 1),
+    ("mix", 3, 1),
+    ("quant_h", 3, 1),
+    ("mix", 5, 1),
+    ("take_direct", 3, 1),
+    ("quant_h", 2, 1),
+    ("mix", 2, 1),
+    ("take_direct", 3, 0),
+    ("mix", 4, 0),
+    ("quant_h", 2, 0),
+    ("quant_h", 3, 0),
+    ("mix", 3, 2),
+    ("mix", 3, 3),
+    ("mix", 5, 2),
+    ("norm", 3),
+    ("mix", 5, 3),
+    ("mix", 2, 2),
+    ("mix", 2, 3),
+    ("mix", 1, 2),
+    ("norm", 5),
+    ("mix", 1, 3),
+    ("mix", 4, 1),
+    ("norm", 2),
+    ("finish_split", 3),
+    ("mix", 4, 2),
+    ("mix", 4, 3),
+    ("mix", 0, 0),
+    ("mix", 0, 1),
+    ("mix", 0, 2),
+    ("mix", 0, 3),
+    ("norm", 1),
+    ("norm", 4),
+    ("finish_split", 5),
+    ("mix", 7, 0),
+    ("mix", 7, 1),
+    ("mix", 7, 2),
+    ("mix", 7, 3),
+    ("gain_z", 2),
+    ("norm", 0),
+    ("gain_z", 1),
+    ("mix", 6, 0),
+    ("finish_gained", 2),
+    ("finish_gained", 1),
+    ("finish_split", 4),
+    ("norm", 7),
+    ("mix", 6, 1),
+    ("gain_z", 0),
+    ("gain_z", 7),
+    ("mix", 6, 2),
+    ("finish_gained", 0),
+    ("mix", 6, 3),
+    ("norm", 6),
+    ("gain_z", 6),
+    ("finish_gained", 7),
+    ("finish_gained", 6),
+]
+BY_SCALAR = {(1, 1)}
+
 
 def tile_grid_to_mesh_mixing_f1_kernel(
     tc, state_bytes, state_scale, gate_words, gate_scales, gate_bias, sun, sun_gain,
@@ -40,12 +274,13 @@ def tile_grid_to_mesh_mixing_f1_kernel(
         mix_s = keep.tile([128, NG, P], U8, name="mix_s", align_bytes=64)
         mesh_sb = keep.tile([128, 8, C], BF16, name="mesh_sb")
         ident = keep.tile([128, 128], F32, name="ident")
-        ident_bf = keep.tile([128, 16], BF16, name="ident_bf")
-        ones = keep.tile([128, 128], BF16, name="ones")
+        ident_bf = keep.tile([128, 128], BF16, name="ident_bf")
+        scale_c = keep.tile([128, 2, 4], F32, name="scale_c")
         vec_rows = keep.tile([128, 128], BF16, name="vec_rows")
-        row0 = keep.tile([128, G + C], BF16, name="row0")
-        sun_b = keep.tile([128, G], F32, name="sun_b")
-        gain_b = keep.tile([128, C], F32, name="gain_b")
+        ones = keep.tile([128, 128], BF16, name="ones")
+        row0 = keep.tile([128, 512], BF16, name="row0")
+        sun_b = [keep.tile([128, 512], BF16, name=f"sun{g}") for g in range(NG)]
+        gain_b = keep.tile([128, C], BF16, name="gain_b")
         cols = keep.tile([128, 16], F32, name="cols")
         area_bf = keep.tile([128, NG, 4], BF16, name="area_bf")
         area_c = keep.tile([128, NG, 4], F32, name="area_c")
@@ -63,38 +298,41 @@ def tile_grid_to_mesh_mixing_f1_kernel(
             for r in range(4):
                 nc.sync.dma_start(out=tile[r:128:32, :, :].bitcast(I32), in_=src[r].bitcast(I32))
 
+        nc.vector.memset(row0[:].bitcast(U32), 0)
+        nc.vector.memset(dummy[:], 0.0)
+        nc.sync.dma_start(out=scale_b[:], in_=state_scale.rearrange("o k -> (o k)").partition_broadcast(128))
         load_state(0, 0, 1)
-        nc.scalar.dma_start(out=scale_b[:], in_=state_scale.rearrange("o k -> (o k)").partition_broadcast(128))
         load_state(0, 1, 2)
         load_state(0, 2, 4)
-        nc.vector.memset(dummy[:], 0.0)
+        nc.scalar.dma_start(out=row0[0:1, :], in_=sun[0:512].rearrange("(o g) -> o g", o=1))
         nc.scalar.activation(out=dummy[:], in_=dummy[:], func=ACT.Silu)
+        nc.vector.memset(ones[:], 1.0)
+        nc.vector.memset(vec_rows[:].bitcast(U32), 0)
         nc.vector.memset(gate_s[:].rearrange("p g n -> p (g n)").bitcast(I32), 0)
         nc.vector.memset(value_s[:].rearrange("p g n -> p (g n)").bitcast(I32), 0)
-        nc.vector.memset(vec_rows[:].bitcast(U32), 0)
-        nc.vector.memset(row0[:].bitcast(U32), 0)
-        nc.vector.memset(mix_s[:].rearrange("p g n -> p (g n)").bitcast(I32), 0)
+        load_state(1, 0, 4)
+        nc.sync.dma_start(out=gate_w[:], in_=gate_words.rearrange("g p n -> p g n"))
+        nc.sync.dma_start(out=value_w[:], in_=value_words.rearrange("g p n -> p g n"))
+        load_scales(gate_s, gate_scales)
+        load_scales(value_s, value_scales)
         make_identity(nc, ident[:])
+        nc.gpsimd.tensor_copy(out=ident_bf[:], in_=ident[:])
         nc.gpsimd.dma_start(out=vec_rows[0:4, :], in_=gate_bias.rearrange("(j c) -> j c", c=128))
         nc.gpsimd.dma_start(out=vec_rows[4:8, :], in_=sun_gain.rearrange("(j c) -> j c", c=128))
         nc.gpsimd.dma_start(out=vec_rows[8:12, :], in_=value_bias.rearrange("(j c) -> j c", c=128))
-        nc.gpsimd.dma_start(out=row0[0:1, 0:G], in_=sun.rearrange("(o g) -> o g", o=1))
-        nc.gpsimd.memset(ones[:], 1.0)
-        nc.gpsimd.tensor_copy(out=ident_bf[:], in_=ident[:, 0:16])
-        nc.gpsimd.dma_start(out=row0[0:1, G : G + C], in_=gain.rearrange("(o g) -> o g", o=1))
+        nc.gpsimd.dma_start(out=scale_c[:], in_=state_scale.rearrange("o (g p t) -> p (o g) t", p=128, t=4))
         nc.gpsimd.dma_start(out=area_bf[:], in_=area.rearrange("(g p t) -> p g t", p=128, t=4))
         nc.gpsimd.memset(mhalf[:], -0.5)
+        nc.gpsimd.memset(mix_s[:].rearrange("p g n -> p (g n)").bitcast(I32), 0)
         nc.gpsimd.tensor_copy(out=area_c[:], in_=area_bf[:])
 
-        load_scales(gate_s, gate_scales)
-        load_scales(value_s, value_scales)
-        nc.sync.dma_start(out=gate_w[:], in_=gate_words.rearrange("g p n -> p g n"))
-        nc.sync.dma_start(out=value_w[:], in_=value_words.rearrange("g p n -> p g n"))
-        load_state(1, 0, 4)
         load_state(2, 0, 4)
-        load_scales(mix_s, mix_scales)
         load_state(3, 0, 4)
+        load_scales(mix_s, mix_scales)
+        for g in range(1, NG):
+            nc.sync.dma_start(out=sun_b[g][:], in_=sun[512 * g : 512 * (g + 1)].partition_broadcast(128))
         nc.sync.dma_start(out=mix_w[:], in_=mix_words.rearrange("g p n -> p g n"))
+        nc.sync.dma_start(out=gain_b[:], in_=gain.partition_broadcast(128))
         nc.sync.dma_start(out=mesh_sb[:], in_=mesh.rearrange("(m p) c -> p m c", p=128))
 
         x_bank, e_bank, h_bank = 2, 4, 2
@@ -104,37 +342,82 @@ def tile_grid_to_mesh_mixing_f1_kernel(
 
         xw, xg, xq, xs = {}, {}, {}, {}
 
+        by_scalar = BY_SCALAR
+
         def widen(g, t):
-            w = work.tile([128, K], BF16, tag="xw", bufs=6, name=f"xw{g}_{t}")
-            nc.vector.tensor_tensor(out=w[:], in0=state_sb[g][:, t, :].bitcast(E4M3), in1=scale_b[:], op=ALU.mult)
+            ks = slice(512 if (g, 0) in by_scalar else 0, 512 if (g, 1) in by_scalar else K)
+            w = work.tile([128, K], BF16, tag="xw", bufs=8, name=f"xw{g}_{t}")
+            nc.vector.tensor_tensor(
+                out=w[:, ks], in0=state_sb[g][:, t, ks].bitcast(E4M3), in1=scale_b[:, ks], op=ALU.mult
+            )
             xw[g, t] = w
 
+        xb = {}
+
         def turn(g, tp):
-            banks = []
             for kg in range(2):
+                if (g, kg) in by_scalar:
+                    continue
                 b = bank("x", x_bank, f"xt{g}_{tp}_{kg}")
                 bv = b[:].rearrange("p (t u r) -> p t u r", t=2, u=2)
                 for t in range(2):
                     words = xw[g, 2 * tp + t][:].bitcast(F32)
                     for u in range(2):
                         nc.tensor.transpose(bv[:, t, u, :], words[:, 256 * kg + u : 256 * (kg + 1) : 2], ident[:])
-                banks.append(bv)
-            return banks
+                xb[g, tp, kg] = bv
 
-        def take(g, tp, banks):
+        def new_xg(g, kg):
+            xg[g, kg] = work.tile([128, 512, 4], BF16, tag=f"xg{kg}", bufs=3, name=f"xg{g}_{kg}", align_bytes=64)
+
+        def take(g, tp):
             for kg in range(2):
-                if tp == 0:
-                    xg[g, kg] = work.tile([128, 512, 4], BF16, tag=f"xg{kg}", bufs=2, name=f"xg{g}_{kg}", align_bytes=64)
+                if (g, kg) in by_scalar:
+                    continue
+                if (g, kg) not in xg:
+                    new_xg(g, kg)
                 dst = xg[g, kg][:, 256 * tp : 256 * (tp + 1), :].rearrange("p c j -> p (c j)").bitcast(F32)
                 nc.scalar.copy(
                     out=dst.rearrange("p (t r u) -> p t r u", t=2, u=2),
-                    in_=banks[kg].rearrange("p t u r -> p t r u"),
+                    in_=xb[g, tp, kg].rearrange("p t u r -> p t r u"),
                 )
 
+        xc, xp = {}, {}
+
+        def cast_s(g, kg, t):
+            if (g, kg) not in xc:
+                xc[g, kg] = work.tile([128, 4, 512], BF16, tag="xc", bufs=2, name=f"xc{g}_{kg}")
+            nc.scalar.copy(out=xc[g, kg][:, t, :], in_=state_sb[g][:, t, 512 * kg : 512 * (kg + 1)].bitcast(E4M3))
+
+        def turn_s(g, kg, half):
+            b = psum.tile([128, 2, 4, 128], BF16, tag="x", bufs=x_bank, name=f"xs{g}_{kg}_{half}")
+            for jj in range(2):
+                for t in range(4):
+                    nc.tensor.transpose(b[:, jj, t, :], xc[g, kg][:, t, 2 * half + jj : 512 : 4], ident_bf[:])
+            xb[g, kg, half, "s"] = b
+
+        def take_s(g, kg, half):
+            if (g, kg) not in xp:
+                xp[g, kg] = work.tile([128, 4, 512], BF16, tag="xp", bufs=2, name=f"xp{g}_{kg}")
+            for jj in range(2):
+                tt = 2 * half + jj
+                nc.scalar.activation(
+                    out=xp[g, kg][:, tt, :], in_=xb[g, kg, half, "s"][:, jj, :, :].rearrange("p t r -> p (t r)"),
+                    func=ACT.Copy, scale=scale_c[:, kg, tt : tt + 1],
+                )
+
+        def weave_x(g, kg, eng):
+            new_xg(g, kg)
+            dst = xg[g, kg][:].rearrange("p (c i) t -> p c t i", i=4)
+            src = xp[g, kg][:].rearrange("p t (c i) -> p c t i", i=4)
+            if eng == "v":
+                nc.vector.tensor_copy(out=dst, in_=src)
+            else:
+                nc.scalar.copy(out=dst, in_=src)
+
         def quant_x(g, kg):
-            if kg == 0:
-                xq[g] = work.tile([128, 2, 512], U32, tag="xq", bufs=2, name=f"xq{g}", align_bytes=64)
-                xs[g] = work.tile([128, 2, 512], U8, tag="xs", bufs=2, name=f"xs{g}", align_bytes=64)
+            if g not in xq:
+                xq[g] = work.tile([128, 2, 512], U32, tag="xq", bufs=3, name=f"xq{g}", align_bytes=64)
+                xs[g] = work.tile([128, 2, 512], U8, tag="xs", bufs=3, name=f"xs{g}", align_bytes=64)
             nc.vector.quantize_mx(
                 out=xq[g][:, kg, :].bitcast(E4M3X4), scales=xs[g][:, kg, :],
                 in_=xg[g, kg][:].rearrange("p c j -> p (c j)"),
@@ -142,8 +425,10 @@ def tile_grid_to_mesh_mixing_f1_kernel(
 
         eb, ub, ah, sh, hh = {}, {}, {}, {}, {}
 
-        def encode(g, j):
+        def encode(g, j, which):
             for store, words, scales, nm in ((eb, gate_w, gate_s, "e"), (ub, value_w, value_s, "u")):
+                if nm != which:
+                    continue
                 b = bank("e", e_bank, f"{nm}{g}_{j}")
                 for kg in range(2):
                     nc.tensor.matmul_mx(
@@ -157,20 +442,21 @@ def tile_grid_to_mesh_mixing_f1_kernel(
                 store[g, j] = b
 
         def add_sun(g, j):
-            a = work.tile([128, 512], F32, tag="a", bufs=3, name=f"a{g}_{j}")
+            a = work.tile([128, 512], F32, tag="a", bufs=4, name=f"a{g}_{j}")
             nc.vector.scalar_tensor_tensor(
-                out=a[:], in0=sun_b[:, 512 * g : 512 * (g + 1)], scalar=cols[:, 4 + j : 5 + j], in1=eb[g, j][:],
+                out=a[:].rearrange("p (t q) -> p t q", t=4), in0=sun_b[g][:].rearrange("p (q t) -> p t q", t=4),
+                scalar=cols[:, 4 + j : 5 + j], in1=eb[g, j][:].rearrange("p (t q) -> p t q", t=4),
                 op0=ALU.mult, op1=ALU.add,
             )
             ah[g, j] = a
 
         def gate(g, j):
-            s = work.tile([128, 512], F32, tag="s", bufs=3, name=f"s{g}_{j}")
+            s = work.tile([128, 512], F32, tag="s", bufs=4, name=f"s{g}_{j}")
             nc.scalar.activation(out=s[:], in_=ah[g, j][:], func=ACT.Silu, bias=cols[:, j : j + 1])
             sh[g, j] = s
 
         def product(g, j):
-            h = work.tile([128, 512], F32, tag="hT", bufs=6, name=f"hT{g}_{j}")
+            h = work.tile([128, 512], F32, tag="hT", bufs=8, name=f"hT{g}_{j}")
             nc.vector.scalar_tensor_tensor(
                 out=h[:], in0=ub[g, j][:], scalar=cols[:, 8 + j : 9 + j], in1=sh[g, j][:], op0=ALU.add, op1=ALU.mult,
             )
@@ -178,24 +464,24 @@ def tile_grid_to_mesh_mixing_f1_kernel(
 
         hbank, hb, hi = {}, {}, {}
 
-        def turn_h(g, hf):
-            for tp in range(2):
-                b = bank("h", h_bank, f"hp{g}_{hf}_{tp}")
-                bv = b[:].rearrange("p (t c) -> p t c", t=2)
-                for t in range(2):
-                    for jj in range(2):
-                        tt = 2 * tp + t
-                        nc.tensor.transpose(
-                            bv[:, t, 128 * jj : 128 * (jj + 1)],
-                            hh[g, 2 * hf + jj][:, 128 * tt : 128 * (tt + 1)], ident[:],
-                        )
-                hbank[g, hf, tp] = bv
+        def turn_h(g, hf, tp):
+            b = bank("h", h_bank, f"hp{g}_{hf}_{tp}")
+            bv = b[:].rearrange("p (t c) -> p t c", t=2)
+            for t in range(2):
+                for jj in range(2):
+                    tt = 2 * tp + t
+                    nc.tensor.transpose(
+                        bv[:, t, 128 * jj : 128 * (jj + 1)],
+                        hh[g, 2 * hf + jj][:, 128 * tt : 128 * (tt + 1)], ident[:],
+                    )
+            hbank[g, hf, "tp", tp] = bv
 
-        def take_h(g, hf):
-            hb[g, hf] = work.tile([128, 4, 256], BF16, tag="hb", bufs=2, name=f"hb{g}_{hf}")
-            for t in range(4):
+        def take_h(g, hf, tp):
+            if (g, hf) not in hb:
+                hb[g, hf] = work.tile([128, 4, 256], BF16, tag="hb", bufs=4, name=f"hb{g}_{hf}")
+            for t in range(2 * tp, 2 * tp + 2):
                 nc.scalar.activation(
-                    out=hb[g, hf][:, t, :], in_=hbank[g, hf, t // 2][:, t % 2, :], func=ACT.Copy,
+                    out=hb[g, hf][:, t, :], in_=hbank[g, hf, "tp", tp][:, t % 2, :], func=ACT.Copy,
                     scale=area_c[:, g, t : t + 1],
                 )
 
@@ -208,8 +494,8 @@ def tile_grid_to_mesh_mixing_f1_kernel(
 
         def take_direct(g, j):
             hf = j // 2
-            if j % 2 == 0:
-                hi[g, hf] = work.tile([128, 256, 4], BF16, tag="hi", bufs=2, name=f"hi{g}_{hf}", align_bytes=64)
+            if (g, hf) not in hi:
+                hi[g, hf] = work.tile([128, 256, 4], BF16, tag="hi", bufs=6, name=f"hi{g}_{hf}", align_bytes=64)
             nc.vector.tensor_tensor(
                 out=hi[g, hf][:, 128 * (j % 2) : 128 * (j % 2 + 1), :],
                 in0=hbank[g, j].rearrange("p t c -> p c t"),
@@ -218,7 +504,7 @@ def tile_grid_to_mesh_mixing_f1_kernel(
             )
 
         def weave_h(g, hf, engine):
-            hi[g, hf] = work.tile([128, 256, 4], BF16, tag="hi", bufs=2, name=f"hi{g}_{hf}", align_bytes=64)
+            hi[g, hf] = work.tile([128, 256, 4], BF16, tag="hi", bufs=6, name=f"hi{g}_{hf}", align_bytes=64)
             dst = hi[g, hf][:].rearrange("p (c i) t -> p c t i", i=4)
             src = hb[g, hf][:].rearrange("p t (c i) -> p c t i", i=4)
             if engine == "v":
@@ -235,8 +521,9 @@ def tile_grid_to_mesh_mixing_f1_kernel(
 
         zb = {}
 
-        def mix(m, g, tag, n):
+        def mix(m, g):
             if g == 0:
+                tag, n = ("x", x_bank) if m < 2 else ("e", e_bank) if m < 6 else ("h", h_bank)
                 zb[m] = bank(tag, n, f"z{m}")
             nc.tensor.matmul_mx(
                 out=zb[m][:],
@@ -250,154 +537,55 @@ def tile_grid_to_mesh_mixing_f1_kernel(
         rinvs = {}
 
         def norm(m):
-            sq = work.tile([128, 512], BF16, tag="sq", bufs=2, name=f"sq{m}")
+            sq = work.tile([128, 512], BF16, tag="sq", bufs=3, name=f"sq{m}")
             ssq = work.tile([128, 1], F32, tag="ssq", bufs=8, name=f"ssq{m}")
             rinv = work.tile([128, 1], F32, tag="rinv", bufs=8, name=f"rinv{m}")
-            nc.scalar.activation(out=sq[:], in_=zb[m][:], func=ACT.Square, accum_out=ssq[:])
+            nc.scalar.activation(out=sq[:], in_=zb[m][:], func=ACT.Square, scale=float(C) ** -0.5, accum_out=ssq[:])
             nc.gpsimd.tensor_tensor(out=rinv[:], in0=ssq[:], in1=mhalf[:], op=ALU.pow)
             rinvs[m] = rinv
 
-        def scale_z(m):
-            y = work.tile([128, 512], F32, tag="y", bufs=4, name=f"y{m}")
-            o = work.tile([128, 512], F32, tag="o", bufs=8, name=f"o{m}")
+        y, o = {}, {}
+
+        def store(m):
+            nc.sync.dma_start(out=out[128 * m : 128 * (m + 1), :], in_=o[m][:])
+
+        def gain_z(m):
+            y[m] = work.tile([128, 512], F32, tag="y", bufs=8, name=f"y{m}")
+            nc.vector.tensor_tensor(out=y[m][:], in0=zb[m][:], in1=gain_b[:], op=ALU.mult)
+
+        def finish_gained(m):
+            o[m] = work.tile([128, 512], F32, tag="o", bufs=8, name=f"o{m}")
             nc.vector.scalar_tensor_tensor(
-                out=y[:], in0=zb[m][:], scalar=rinvs[m][:], in1=gain_b[:], op0=ALU.mult, op1=ALU.mult,
+                out=o[m][:], in0=y[m][:], scalar=rinvs[m][:], in1=mesh_sb[:, m, :], op0=ALU.mult, op1=ALU.add,
             )
-            ys[m] = y
-            outs[m] = o
+            store(m)
 
-        ys, outs = {}, {}
-
-        def add_mesh(m, eng):
-            eng.tensor_tensor(out=outs[m][:], in0=ys[m][:], in1=mesh_sb[:, m, :], op=ALU.add)
-            nc.sync.dma_start(out=out[128 * m : 128 * (m + 1), :], in_=outs[m][:])
+        def finish_split(m):
+            y[m] = work.tile([128, 512], F32, tag="y", bufs=8, name=f"y{m}")
+            o[m] = work.tile([128, 512], F32, tag="o", bufs=8, name=f"o{m}")
+            nc.vector.scalar_tensor_tensor(
+                out=y[m][:], in0=zb[m][:], scalar=rinvs[m][:], in1=gain_b[:], op0=ALU.mult, op1=ALU.mult,
+            )
+            nc.gpsimd.tensor_tensor(out=o[m][:], in0=y[m][:], in1=mesh_sb[:, m, :], op=ALU.add)
+            store(m)
 
         def spread_vectors():
             ps = bank("h", h_bank, "vec_ps")
-            nc.tensor.matmul(ps[:, 0:16], lhsT=vec_rows[:], rhs=ident_bf[:], start=True, stop=True)
+            nc.tensor.matmul(ps[:, 0:16], lhsT=vec_rows[:], rhs=ident_bf[:, 0:16], start=True, stop=True)
             nc.scalar.copy(out=cols[:], in_=ps[:, 0:16])
-            for g in range(NG):
-                ps = bank("e", e_bank, f"sun_ps{g}")
-                nc.tensor.matmul(ps[:], lhsT=ones[:], rhs=row0[:, 512 * g : 512 * (g + 1)], start=True, stop=True)
-                nc.scalar.copy(
-                    out=sun_b[:, 512 * g : 512 * (g + 1)].rearrange("p (t q) -> p t q", t=4),
-                    in_=ps[:].rearrange("p (q t) -> p t q", t=4),
-                )
-            ps = bank("h", h_bank, "gain_ps")
-            nc.tensor.matmul(ps[:], lhsT=ones[:], rhs=row0[:, G : G + C], start=True, stop=True)
-            nc.scalar.activation(out=gain_b[:], in_=ps[:], func=ACT.Copy, scale=math_sqrt_c())
 
-        with tc.manual_schedule(engines={mybir.EngineType.PE, mybir.EngineType.DVE, mybir.EngineType.Activation}):
-            widen(0, 0)
-            widen(0, 1)
-            b = turn(0, 0)
-            take(0, 0, b)
-            widen(0, 2)
-            widen(0, 3)
-            b = turn(0, 1)
-            take(0, 1, b)
-            spread_vectors()
-            widen(1, 0)
-            quant_x(0, 0)
-            widen(1, 1)
-            quant_x(0, 1)
-            b = turn(1, 0)
-            take(1, 0, b)
-            encode(0, 0)
-            for g in range(NG - 1):
-                n, n2 = g + 1, g + 2
-                encode(g, 1)
-                add_sun(g, 0)
-                gate(g, 0)
-                if g > 0:
-                    turn_h(g - 1, 1)
-                    take_h(g - 1, 1)
-                widen(n, 2)
-                add_sun(g, 1)
-                gate(g, 1)
-                product(g, 0)
-                if g > 0:
-                    weave_h(g - 1, 1, "a")
-                encode(g, 2)
-                widen(n, 3)
-                product(g, 1)
-                b = turn(n, 1)
-                encode(g, 3)
-                add_sun(g, 2)
-                gate(g, 2)
-                take(n, 1, b)
-                if n2 < NG:
-                    widen(n2, 0)
-                add_sun(g, 3)
-                gate(g, 3)
-                turn_h(g, 0)
-                take_h(g, 0)
-                if g > 0:
-                    quant_h(g - 1, 1)
-                quant_x(n, 0)
-                quant_x(n, 1)
-                product(g, 2)
-                weave_h(g, 0, "a" if n2 < NG else "v")
-                encode(n, 0)
-                if n2 < NG:
-                    widen(n2, 1)
-                product(g, 3)
-                if n2 < NG:
-                    b = turn(n2, 0)
-                    take(n2, 0, b)
-                quant_h(g, 0)
-            g = NG - 1
-            encode(g, 1)
-            turn_h(g - 1, 1)
-            add_sun(g, 0)
-            gate(g, 0)
-            add_sun(g, 1)
-            take_h(g - 1, 1)
-            gate(g, 1)
-            product(g, 0)
-            for m in range(2):
-                for gg in range(2):
-                    mix(m, gg, "x", x_bank)
-            encode(g, 2)
-            weave_h(g - 1, 1, "v")
-            product(g, 1)
-            add_sun(g, 2)
-            gate(g, 2)
-            encode(g, 3)
-            turn_direct(g, 0)
-            turn_direct(g, 1)
-            quant_h(g - 1, 1)
-            add_sun(g, 3)
-            gate(g, 3)
-            take_direct(g, 0)
-            product(g, 2)
-            for m in range(2):
-                mix(m, 2, "x", x_bank)
-            turn_direct(g, 2)
-            for gg in range(3):
-                mix(2, gg, "e", e_bank)
-            take_direct(g, 1)
-            product(g, 3)
-            quant_h(g, 0)
-            turn_direct(g, 3)
-            take_direct(g, 2)
-            for gg in range(3):
-                mix(3, gg, "e", e_bank)
-            take_direct(g, 3)
-            quant_h(g, 1)
-            for m in range(4):
-                mix(m, 3, "e", e_bank)
-            for m in range(4, 8):
-                for gg in range(NG):
-                    mix(m, gg, "e" if m < 6 else "h", e_bank if m < 6 else h_bank)
-            ahead = 3
-            for m in range(8 + ahead):
-                if m < 8:
-                    norm(m)
-                if m >= ahead:
-                    scale_z(m - ahead)
-                    add_mesh(m - ahead, nc.gpsimd if (m - ahead) % 2 == 1 else nc.vector)
+        def spread_sun(g):
+            ps = bank("h", h_bank, f"sun_ps{g}")
+            nc.tensor.matmul(ps[:], lhsT=ones[:], rhs=row0[:], start=True, stop=True)
+            nc.scalar.copy(out=sun_b[g][:], in_=ps[:])
 
-
-def math_sqrt_c():
-    return float(C) ** 0.5
+        with tc.manual_schedule():
+            table = dict(
+                widen=widen, cast_s=cast_s, turn=turn, take=take, turn_s=turn_s, take_s=take_s, weave_x=weave_x,
+                quant_x=quant_x, encode=encode, add_sun=add_sun, gate=gate, product=product, turn_h=turn_h,
+                take_h=take_h, turn_direct=turn_direct, take_direct=take_direct, weave_h=weave_h, quant_h=quant_h,
+                mix=mix, norm=norm, gain_z=gain_z, finish_gained=finish_gained, finish_split=finish_split,
+                spread_vectors=spread_vectors, spread_sun=spread_sun,
+            )
+            for name, *args in PLAN:
+                table[name](*args)

from contextlib import ExitStack

import concourse.mybir as mybir
from concourse.masks import make_identity

G, K, C, P = 2048, 1024, 512, 1024
FLOPS = 2 * G * K * C * 2 + 2 * G * P * C

F32 = mybir.dt.float32
BF16 = mybir.dt.bfloat16
U8 = mybir.dt.uint8
U32 = mybir.dt.uint32
I32 = mybir.dt.int32
E4M3 = mybir.dt.float8_e4m3fn
E4M3X4 = mybir.dt.float8_e4m3fn_x4
E2M1X4 = mybir.dt.float4_e2m1fn_x4
ALU = mybir.AluOpType
ACT = mybir.ActivationFunctionType

NG = 4

PLAN = [
    ("widen", 0, 0),
    ("spread_sun", 0),
    ("cast_s", 1, 1, 1),
    ("widen", 0, 1),
    ("widen", 0, 2),
    ("cast_s", 1, 1, 3),
    ("widen", 0, 3),
    ("turn", 0, 0),
    ("widen", 1, 2),
    ("take", 0, 0),
    ("widen", 1, 0),
    ("turn", 0, 1),
    ("cast_s", 1, 1, 0),
    ("cast_s", 1, 1, 2),
    ("take", 0, 1),
    ("widen", 1, 1),
    ("turn_s", 1, 1, 1),
    ("widen", 1, 3),
    ("turn_s", 1, 1, 0),
    ("quant_x", 0, 0),
    ("widen", 2, 1),
    ("take_s", 1, 1, 1),
    ("widen", 2, 3),
    ("take_s", 1, 1, 0),
    ("quant_x", 0, 1),
    ("spread_vectors",),
    ("encode", 0, 0, "e"),
    ("encode", 0, 1, "e"),
    ("encode", 0, 3, "e"),
    ("encode", 0, 2, "e"),
    ("widen", 2, 0),
    ("turn", 1, 1),
    ("turn", 1, 0),
    ("add_sun", 0, 0),
    ("weave_x", 1, 1, "a"),
    ("take", 1, 1),
    ("add_sun", 0, 1),
    ("encode", 0, 3, "u"),
    ("add_sun", 0, 3),
    ("take", 1, 0),
    ("widen", 3, 0),
    ("quant_x", 1, 1),
    ("encode", 0, 2, "u"),
    ("turn", 2, 0),
    ("add_sun", 0, 2),
    ("quant_x", 1, 0),
    ("encode", 1, 3, "e"),
    ("gate", 0, 3),
    ("encode", 1, 2, "e"),
    ("gate", 0, 0),
    ("product", 0, 3),
    ("gate", 0, 2),
    ("product", 0, 2),
    ("add_sun", 1, 3),
    ("turn_h", 0, 1, 1),
    ("turn_h", 0, 1, 0),
    ("take", 2, 0),
    ("encode", 0, 1, "u"),
    ("gate", 0, 1),
    ("take_h", 0, 1, 0),
    ("widen", 2, 2),
    ("add_sun", 1, 2),
    ("encode", 0, 0, "u"),
    ("take_h", 0, 1, 1),
    ("product", 0, 1),
    ("gate", 1, 3),
    ("product", 0, 0),
    ("weave_h", 0, 1, "a"),
    ("encode", 1, 0, "e"),
    ("encode", 1, 1, "e"),
    ("add_sun", 1, 0),
    ("turn", 2, 1),
    ("turn_h", 0, 0, 1),
    ("turn_h", 0, 0, 0),
    ("add_sun", 1, 1),
    ("take", 2, 1),
    ("take_h", 0, 0, 1),
    ("take_h", 0, 0, 0),
    ("encode", 1, 3, "u"),
    ("widen", 3, 2),
    ("gate", 1, 2),
    ("widen", 3, 1),
    ("encode", 1, 2, "u"),
    ("encode", 1, 0, "u"),
    ("encode", 1, 1, "u"),
    ("quant_x", 2, 0),
    ("product", 1, 3),
    ("gate", 1, 0),
    ("product", 1, 2),
    ("turn", 3, 0),
    ("turn_h", 1, 1, 0),
    ("gate", 1, 1),
    ("weave_h", 0, 0, "a"),
    ("quant_x", 2, 1),
    ("encode", 2, 1, "e"),
    ("product", 1, 0),
    ("product", 1, 1),
    ("take", 3, 0),
    ("add_sun", 2, 1),
    ("encode", 2, 2, "e"),
    ("add_sun", 2, 2),
    ("widen", 3, 3),
    ("encode", 2, 0, "e"),
    ("take_h", 1, 1, 0),
    ("encode", 2, 3, "e"),
    ("gate", 2, 1),
    ("turn_h", 1, 0, 0),
    ("add_sun", 2, 0),
    ("gate", 2, 2),
    ("take_h", 1, 0, 0),
    ("quant_h", 0, 0),
    ("add_sun", 2, 3),
    ("turn_h", 1, 1, 1),
    ("turn", 3, 1),
    ("take", 3, 1),
    ("gate", 2, 3),
    ("encode", 2, 3, "u"),
    ("quant_x", 3, 0),
    ("take_h", 1, 1, 1),
    ("encode", 2, 2, "u"),
    ("turn_h", 1, 0, 1),
    ("take_h", 1, 0, 1),
    ("quant_x", 3, 1),
    ("product", 2, 3),
    ("encode", 3, 1, "e"),
    ("product", 2, 2),
    ("encode", 2, 0, "u"),
    ("gate", 2, 0),
    ("encode", 3, 2, "e"),
    ("encode", 2, 1, "u"),
    ("turn_h", 2, 1, 0),
    ("turn_h", 2, 1, 1),
    ("weave_h", 1, 1, "a"),
    ("take_h", 2, 1, 0),
    ("add_sun", 3, 1),
    ("take_h", 2, 1, 1),
    ("product", 2, 0),
    ("product", 2, 1),
    ("encode", 3, 0, "e"),
    ("add_sun", 3, 2),
    ("quant_h", 0, 1),
    ("encode", 3, 3, "e"),
    ("quant_h", 1, 1),
    ("add_sun", 3, 0),
    ("add_sun", 3, 3),
    ("gate", 3, 2),
    ("gate", 3, 1),
    ("gate", 3, 0),
    ("encode", 3, 2, "u"),
    ("product", 3, 2),
    ("gate", 3, 3),
    ("encode", 3, 3, "u"),
    ("turn_h", 2, 0, 0),
    ("turn_direct", 3, 2),
    ("encode", 3, 1, "u"),
    ("take_h", 2, 0, 0),
    ("mix", 1, 0),
    ("product", 3, 3),
    ("weave_h", 1, 0, "a"),
    ("turn_h", 2, 0, 1),
    ("take_direct", 3, 2),
    ("turn_direct", 3, 3),
    ("take_h", 2, 0, 1),
    ("encode", 3, 0, "u"),
    ("mix", 2, 0),
    ("mix", 3, 0),
    ("weave_h", 2, 1, "a"),
    ("product", 3, 1),
    ("turn_direct", 3, 1),
    ("take_direct", 3, 3),
    ("product", 3, 0),
    ("turn_direct", 3, 0),
    ("mix", 5, 0),
    ("quant_h", 1, 0),
    ("weave_h", 2, 0, "a"),
    ("mix", 1, 1),
    ("mix", 3, 1),
    ("quant_h", 3, 1),
    ("mix", 5, 1),
    ("take_direct", 3, 1),
    ("quant_h", 2, 1),
    ("mix", 2, 1),
    ("take_direct", 3, 0),
    ("mix", 4, 0),
    ("quant_h", 2, 0),
    ("quant_h", 3, 0),
    ("mix", 3, 2),
    ("mix", 3, 3),
    ("mix", 5, 2),
    ("norm", 3),
    ("mix", 5, 3),
    ("mix", 2, 2),
    ("mix", 2, 3),
    ("mix", 1, 2),
    ("norm", 5),
    ("mix", 1, 3),
    ("mix", 4, 1),
    ("norm", 2),
    ("finish_split", 3),
    ("mix", 4, 2),
    ("mix", 4, 3),
    ("mix", 0, 0),
    ("mix", 0, 1),
    ("mix", 0, 2),
    ("mix", 0, 3),
    ("norm", 1),
    ("norm", 4),
    ("finish_split", 5),
    ("mix", 7, 0),
    ("mix", 7, 1),
    ("mix", 7, 2),
    ("mix", 7, 3),
    ("gain_z", 2),
    ("norm", 0),
    ("gain_z", 1),
    ("mix", 6, 0),
    ("finish_gained", 2),
    ("finish_gained", 1),
    ("finish_split", 4),
    ("norm", 7),
    ("mix", 6, 1),
    ("gain_z", 0),
    ("gain_z", 7),
    ("mix", 6, 2),
    ("finish_gained", 0),
    ("mix", 6, 3),
    ("norm", 6),
    ("gain_z", 6),
    ("finish_gained", 7),
    ("finish_gained", 6),
]
BY_SCALAR = {(1, 1)}


def tile_grid_to_mesh_mixing_f1_kernel(
    tc, state_bytes, state_scale, gate_words, gate_scales, gate_bias, sun, sun_gain,
    value_words, value_scales, value_bias, area, mix_words, mix_scales, mesh, gain, out,
):
    nc = tc.nc
    with ExitStack() as ctx:
        keep = ctx.enter_context(tc.tile_pool(name="keep", bufs=1))
        work = ctx.enter_context(tc.tile_pool(name="work", bufs=2))
        psum = ctx.enter_context(tc.psum_pool(name="psum", bufs=1))

        state_sb = [keep.tile([128, 4, K], U8, name=f"state{g}", align_bytes=64) for g in range(NG)]
        scale_b = keep.tile([128, K], F32, name="scale_b")
        gate_w = keep.tile([128, 2, 2 * C], U8, name="gate_w", align_bytes=64)
        value_w = keep.tile([128, 2, 2 * C], U8, name="value_w", align_bytes=64)
        gate_s = keep.tile([128, 2, C], U8, name="gate_s", align_bytes=64)
        value_s = keep.tile([128, 2, C], U8, name="value_s", align_bytes=64)
        mix_w = keep.tile([128, NG, 2 * P], U8, name="mix_w", align_bytes=64)
        mix_s = keep.tile([128, NG, P], U8, name="mix_s", align_bytes=64)
        mesh_sb = keep.tile([128, 8, C], BF16, name="mesh_sb")
        ident = keep.tile([128, 128], F32, name="ident")
        ident_bf = keep.tile([128, 128], BF16, name="ident_bf")
        scale_c = keep.tile([128, 2, 4], F32, name="scale_c")
        vec_rows = keep.tile([128, 128], BF16, name="vec_rows")
        ones = keep.tile([128, 128], BF16, name="ones")
        row0 = keep.tile([128, 512], BF16, name="row0")
        sun_b = [keep.tile([128, 512], BF16, name=f"sun{g}") for g in range(NG)]
        gain_b = keep.tile([128, C], BF16, name="gain_b")
        cols = keep.tile([128, 16], F32, name="cols")
        area_bf = keep.tile([128, NG, 4], BF16, name="area_bf")
        area_c = keep.tile([128, NG, 4], F32, name="area_c")
        dummy = keep.tile([128, 1], F32, name="dummy")
        mhalf = keep.tile([128, 1], F32, name="mhalf")
        h_codes = keep.tile([128, NG, C], U32, name="h_codes", align_bytes=64)
        h_scales = keep.tile([128, NG, C], U8, name="h_scales", align_bytes=64)

        def load_state(g, t0, t1):
            src = state_bytes[512 * g : 512 * (g + 1), :].rearrange("(p t) k -> p t k", t=4)
            nc.sync.dma_start(out=state_sb[g][:, t0:t1, :], in_=src[:, t0:t1, :])

        def load_scales(tile, dram):
            src = dram.rearrange("g (q r) n -> r q g n", r=4)
            for r in range(4):
                nc.sync.dma_start(out=tile[r:128:32, :, :].bitcast(I32), in_=src[r].bitcast(I32))

        nc.vector.memset(row0[:].bitcast(U32), 0)
        nc.vector.memset(dummy[:], 0.0)
        nc.sync.dma_start(out=scale_b[:], in_=state_scale.rearrange("o k -> (o k)").partition_broadcast(128))
        load_state(0, 0, 1)
        load_state(0, 1, 2)
        load_state(0, 2, 4)
        nc.scalar.dma_start(out=row0[0:1, :], in_=sun[0:512].rearrange("(o g) -> o g", o=1))
        nc.scalar.activation(out=dummy[:], in_=dummy[:], func=ACT.Silu)
        nc.vector.memset(ones[:], 1.0)
        nc.vector.memset(vec_rows[:].bitcast(U32), 0)
        nc.vector.memset(gate_s[:].rearrange("p g n -> p (g n)").bitcast(I32), 0)
        nc.vector.memset(value_s[:].rearrange("p g n -> p (g n)").bitcast(I32), 0)
        load_state(1, 0, 4)
        nc.sync.dma_start(out=gate_w[:], in_=gate_words.rearrange("g p n -> p g n"))
        nc.sync.dma_start(out=value_w[:], in_=value_words.rearrange("g p n -> p g n"))
        load_scales(gate_s, gate_scales)
        load_scales(value_s, value_scales)
        make_identity(nc, ident[:])
        nc.gpsimd.tensor_copy(out=ident_bf[:], in_=ident[:])
        nc.gpsimd.dma_start(out=vec_rows[0:4, :], in_=gate_bias.rearrange("(j c) -> j c", c=128))
        nc.gpsimd.dma_start(out=vec_rows[4:8, :], in_=sun_gain.rearrange("(j c) -> j c", c=128))
        nc.gpsimd.dma_start(out=vec_rows[8:12, :], in_=value_bias.rearrange("(j c) -> j c", c=128))
        nc.gpsimd.dma_start(out=scale_c[:], in_=state_scale.rearrange("o (g p t) -> p (o g) t", p=128, t=4))
        nc.gpsimd.dma_start(out=area_bf[:], in_=area.rearrange("(g p t) -> p g t", p=128, t=4))
        nc.gpsimd.memset(mhalf[:], -0.5)
        nc.gpsimd.memset(mix_s[:].rearrange("p g n -> p (g n)").bitcast(I32), 0)
        nc.gpsimd.tensor_copy(out=area_c[:], in_=area_bf[:])

        load_state(2, 0, 4)
        load_state(3, 0, 4)
        load_scales(mix_s, mix_scales)
        for g in range(1, NG):
            nc.sync.dma_start(out=sun_b[g][:], in_=sun[512 * g : 512 * (g + 1)].partition_broadcast(128))
        nc.sync.dma_start(out=mix_w[:], in_=mix_words.rearrange("g p n -> p g n"))
        nc.sync.dma_start(out=gain_b[:], in_=gain.partition_broadcast(128))
        nc.sync.dma_start(out=mesh_sb[:], in_=mesh.rearrange("(m p) c -> p m c", p=128))

        x_bank, e_bank, h_bank = 2, 4, 2

        def bank(tag, n, name):
            return psum.tile([128, 512], F32, tag=tag, bufs=n, name=name)

        xw, xg, xq, xs = {}, {}, {}, {}

        by_scalar = BY_SCALAR

        def widen(g, t):
            ks = slice(512 if (g, 0) in by_scalar else 0, 512 if (g, 1) in by_scalar else K)
            w = work.tile([128, K], BF16, tag="xw", bufs=8, name=f"xw{g}_{t}")
            nc.vector.tensor_tensor(
                out=w[:, ks], in0=state_sb[g][:, t, ks].bitcast(E4M3), in1=scale_b[:, ks], op=ALU.mult
            )
            xw[g, t] = w

        xb = {}

        def turn(g, tp):
            for kg in range(2):
                if (g, kg) in by_scalar:
                    continue
                b = bank("x", x_bank, f"xt{g}_{tp}_{kg}")
                bv = b[:].rearrange("p (t u r) -> p t u r", t=2, u=2)
                for t in range(2):
                    words = xw[g, 2 * tp + t][:].bitcast(F32)
                    for u in range(2):
                        nc.tensor.transpose(bv[:, t, u, :], words[:, 256 * kg + u : 256 * (kg + 1) : 2], ident[:])
                xb[g, tp, kg] = bv

        def new_xg(g, kg):
            xg[g, kg] = work.tile([128, 512, 4], BF16, tag=f"xg{kg}", bufs=3, name=f"xg{g}_{kg}", align_bytes=64)

        def take(g, tp):
            for kg in range(2):
                if (g, kg) in by_scalar:
                    continue
                if (g, kg) not in xg:
                    new_xg(g, kg)
                dst = xg[g, kg][:, 256 * tp : 256 * (tp + 1), :].rearrange("p c j -> p (c j)").bitcast(F32)
                nc.scalar.copy(
                    out=dst.rearrange("p (t r u) -> p t r u", t=2, u=2),
                    in_=xb[g, tp, kg].rearrange("p t u r -> p t r u"),
                )

        xc, xp = {}, {}

        def cast_s(g, kg, t):
            if (g, kg) not in xc:
                xc[g, kg] = work.tile([128, 4, 512], BF16, tag="xc", bufs=2, name=f"xc{g}_{kg}")
            nc.scalar.copy(out=xc[g, kg][:, t, :], in_=state_sb[g][:, t, 512 * kg : 512 * (kg + 1)].bitcast(E4M3))

        def turn_s(g, kg, half):
            b = psum.tile([128, 2, 4, 128], BF16, tag="x", bufs=x_bank, name=f"xs{g}_{kg}_{half}")
            for jj in range(2):
                for t in range(4):
                    nc.tensor.transpose(b[:, jj, t, :], xc[g, kg][:, t, 2 * half + jj : 512 : 4], ident_bf[:])
            xb[g, kg, half, "s"] = b

        def take_s(g, kg, half):
            if (g, kg) not in xp:
                xp[g, kg] = work.tile([128, 4, 512], BF16, tag="xp", bufs=2, name=f"xp{g}_{kg}")
            for jj in range(2):
                tt = 2 * half + jj
                nc.scalar.activation(
                    out=xp[g, kg][:, tt, :], in_=xb[g, kg, half, "s"][:, jj, :, :].rearrange("p t r -> p (t r)"),
                    func=ACT.Copy, scale=scale_c[:, kg, tt : tt + 1],
                )

        def weave_x(g, kg, eng):
            new_xg(g, kg)
            dst = xg[g, kg][:].rearrange("p (c i) t -> p c t i", i=4)
            src = xp[g, kg][:].rearrange("p t (c i) -> p c t i", i=4)
            if eng == "v":
                nc.vector.tensor_copy(out=dst, in_=src)
            else:
                nc.scalar.copy(out=dst, in_=src)

        def quant_x(g, kg):
            if g not in xq:
                xq[g] = work.tile([128, 2, 512], U32, tag="xq", bufs=3, name=f"xq{g}", align_bytes=64)
                xs[g] = work.tile([128, 2, 512], U8, tag="xs", bufs=3, name=f"xs{g}", align_bytes=64)
            nc.vector.quantize_mx(
                out=xq[g][:, kg, :].bitcast(E4M3X4), scales=xs[g][:, kg, :],
                in_=xg[g, kg][:].rearrange("p c j -> p (c j)"),
            )

        eb, ub, ah, sh, hh = {}, {}, {}, {}, {}

        def encode(g, j, which):
            for store, words, scales, nm in ((eb, gate_w, gate_s, "e"), (ub, value_w, value_s, "u")):
                if nm != which:
                    continue
                b = bank("e", e_bank, f"{nm}{g}_{j}")
                for kg in range(2):
                    nc.tensor.matmul_mx(
                        out=b[:],
                        lhsT=words[:, kg, 256 * j : 256 * (j + 1)].bitcast(E2M1X4),
                        lhsT_scale=scales[:, kg, 128 * j : 128 * (j + 1)],
                        rhs=xq[g][:, kg, :].bitcast(E4M3X4),
                        rhs_scale=xs[g][:, kg, :],
                        start=(kg == 0), stop=(kg == 1),
                    )
                store[g, j] = b

        def add_sun(g, j):
            a = work.tile([128, 512], F32, tag="a", bufs=4, name=f"a{g}_{j}")
            nc.vector.scalar_tensor_tensor(
                out=a[:].rearrange("p (t q) -> p t q", t=4), in0=sun_b[g][:].rearrange("p (q t) -> p t q", t=4),
                scalar=cols[:, 4 + j : 5 + j], in1=eb[g, j][:].rearrange("p (t q) -> p t q", t=4),
                op0=ALU.mult, op1=ALU.add,
            )
            ah[g, j] = a

        def gate(g, j):
            s = work.tile([128, 512], F32, tag="s", bufs=4, name=f"s{g}_{j}")
            nc.scalar.activation(out=s[:], in_=ah[g, j][:], func=ACT.Silu, bias=cols[:, j : j + 1])
            sh[g, j] = s

        def product(g, j):
            h = work.tile([128, 512], F32, tag="hT", bufs=8, name=f"hT{g}_{j}")
            nc.vector.scalar_tensor_tensor(
                out=h[:], in0=ub[g, j][:], scalar=cols[:, 8 + j : 9 + j], in1=sh[g, j][:], op0=ALU.add, op1=ALU.mult,
            )
            hh[g, j] = h

        hbank, hb, hi = {}, {}, {}

        def turn_h(g, hf, tp):
            b = bank("h", h_bank, f"hp{g}_{hf}_{tp}")
            bv = b[:].rearrange("p (t c) -> p t c", t=2)
            for t in range(2):
                for jj in range(2):
                    tt = 2 * tp + t
                    nc.tensor.transpose(
                        bv[:, t, 128 * jj : 128 * (jj + 1)],
                        hh[g, 2 * hf + jj][:, 128 * tt : 128 * (tt + 1)], ident[:],
                    )
            hbank[g, hf, "tp", tp] = bv

        def take_h(g, hf, tp):
            if (g, hf) not in hb:
                hb[g, hf] = work.tile([128, 4, 256], BF16, tag="hb", bufs=4, name=f"hb{g}_{hf}")
            for t in range(2 * tp, 2 * tp + 2):
                nc.scalar.activation(
                    out=hb[g, hf][:, t, :], in_=hbank[g, hf, "tp", tp][:, t % 2, :], func=ACT.Copy,
                    scale=area_c[:, g, t : t + 1],
                )

        def turn_direct(g, j):
            b = bank("h", h_bank, f"hd{g}_{j}")
            bv = b[:].rearrange("p (t c) -> p t c", t=4)
            for t in range(4):
                nc.tensor.transpose(bv[:, t, :], hh[g, j][:, 128 * t : 128 * (t + 1)], ident[:])
            hbank[g, j] = bv

        def take_direct(g, j):
            hf = j // 2
            if (g, hf) not in hi:
                hi[g, hf] = work.tile([128, 256, 4], BF16, tag="hi", bufs=6, name=f"hi{g}_{hf}", align_bytes=64)
            nc.vector.tensor_tensor(
                out=hi[g, hf][:, 128 * (j % 2) : 128 * (j % 2 + 1), :],
                in0=hbank[g, j].rearrange("p t c -> p c t"),
                in1=area_c[:, g, :].unsqueeze(1).to_broadcast([128, 128, 4]),
                op=ALU.mult,
            )

        def weave_h(g, hf, engine):
            hi[g, hf] = work.tile([128, 256, 4], BF16, tag="hi", bufs=6, name=f"hi{g}_{hf}", align_bytes=64)
            dst = hi[g, hf][:].rearrange("p (c i) t -> p c t i", i=4)
            src = hb[g, hf][:].rearrange("p t (c i) -> p c t i", i=4)
            if engine == "v":
                nc.vector.tensor_copy(out=dst, in_=src)
            else:
                nc.scalar.copy(out=dst, in_=src)

        def quant_h(g, hf):
            cs = slice(256 * hf, 256 * (hf + 1))
            nc.vector.quantize_mx(
                out=h_codes[:, g, cs].bitcast(E4M3X4), scales=h_scales[:, g, cs],
                in_=hi[g, hf][:].rearrange("p c t -> p (c t)"),
            )

        zb = {}

        def mix(m, g):
            if g == 0:
                tag, n = ("x", x_bank) if m < 2 else ("e", e_bank) if m < 6 else ("h", h_bank)
                zb[m] = bank(tag, n, f"z{m}")
            nc.tensor.matmul_mx(
                out=zb[m][:],
                lhsT=mix_w[:, g, 256 * m : 256 * (m + 1)].bitcast(E2M1X4),
                lhsT_scale=mix_s[:, g, 128 * m : 128 * (m + 1)],
                rhs=h_codes[:, g, :].bitcast(E4M3X4),
                rhs_scale=h_scales[:, g, :],
                start=(g == 0), stop=(g == NG - 1),
            )

        rinvs = {}

        def norm(m):
            sq = work.tile([128, 512], BF16, tag="sq", bufs=3, name=f"sq{m}")
            ssq = work.tile([128, 1], F32, tag="ssq", bufs=8, name=f"ssq{m}")
            rinv = work.tile([128, 1], F32, tag="rinv", bufs=8, name=f"rinv{m}")
            nc.scalar.activation(out=sq[:], in_=zb[m][:], func=ACT.Square, scale=float(C) ** -0.5, accum_out=ssq[:])
            nc.gpsimd.tensor_tensor(out=rinv[:], in0=ssq[:], in1=mhalf[:], op=ALU.pow)
            rinvs[m] = rinv

        y, o = {}, {}

        def store(m):
            nc.sync.dma_start(out=out[128 * m : 128 * (m + 1), :], in_=o[m][:])

        def gain_z(m):
            y[m] = work.tile([128, 512], F32, tag="y", bufs=8, name=f"y{m}")
            nc.vector.tensor_tensor(out=y[m][:], in0=zb[m][:], in1=gain_b[:], op=ALU.mult)

        def finish_gained(m):
            o[m] = work.tile([128, 512], F32, tag="o", bufs=8, name=f"o{m}")
            nc.vector.scalar_tensor_tensor(
                out=o[m][:], in0=y[m][:], scalar=rinvs[m][:], in1=mesh_sb[:, m, :], op0=ALU.mult, op1=ALU.add,
            )
            store(m)

        def finish_split(m):
            y[m] = work.tile([128, 512], F32, tag="y", bufs=8, name=f"y{m}")
            o[m] = work.tile([128, 512], F32, tag="o", bufs=8, name=f"o{m}")
            nc.vector.scalar_tensor_tensor(
                out=y[m][:], in0=zb[m][:], scalar=rinvs[m][:], in1=gain_b[:], op0=ALU.mult, op1=ALU.mult,
            )
            nc.gpsimd.tensor_tensor(out=o[m][:], in0=y[m][:], in1=mesh_sb[:, m, :], op=ALU.add)
            store(m)

        def spread_vectors():
            ps = bank("h", h_bank, "vec_ps")
            nc.tensor.matmul(ps[:, 0:16], lhsT=vec_rows[:], rhs=ident_bf[:, 0:16], start=True, stop=True)
            nc.scalar.copy(out=cols[:], in_=ps[:, 0:16])

        def spread_sun(g):
            ps = bank("h", h_bank, f"sun_ps{g}")
            nc.tensor.matmul(ps[:], lhsT=ones[:], rhs=row0[:], start=True, stop=True)
            nc.scalar.copy(out=sun_b[g][:], in_=ps[:])

        with tc.manual_schedule():
            table = dict(
                widen=widen, cast_s=cast_s, turn=turn, take=take, turn_s=turn_s, take_s=take_s, weave_x=weave_x,
                quant_x=quant_x, encode=encode, add_sun=add_sun, gate=gate, product=product, turn_h=turn_h,
                take_h=take_h, turn_direct=turn_direct, take_direct=take_direct, weave_h=weave_h, quant_h=quant_h,
                mix=mix, norm=norm, gain_z=gain_z, finish_gained=finish_gained, finish_split=finish_split,
                spread_vectors=spread_vectors, spread_sun=spread_sun,
            )
            for name, *args in PLAN:
                table[name](*args)
